import numpy as np
import ml_dtypes


def mxq(x, axis, fmt="e4m3"):
    dtype, down = {"e4m3": (ml_dtypes.float8_e4m3fn, 7), "e5m2": (ml_dtypes.float8_e5m2, 14)}[fmt]
    v = np.moveaxis(np.asarray(x, np.float32).astype(ml_dtypes.bfloat16).astype(np.float64), axis, -1)
    blocks = v.reshape(v.shape[:-1] + (-1, 32))
    amax = np.abs(blocks).max(-1, keepdims=True)
    byte = np.maximum(np.where(amax > 0, np.frexp(amax)[1] - 1 + 127, 0) - down, 1)
    scale = np.exp2(byte - 127.0)
    codes = (blocks / scale).astype(np.float32).astype(dtype).astype(np.float64)
    return np.moveaxis((codes * scale).reshape(v.shape), -1, axis)


WIDE = False


def mx_kscale(k):
    if not WIDE:
        return np.ones(k)
    levels = np.array([30, -30])
    if k % 512:
        return np.exp2(np.random.permutation(np.resize(levels, k // 32))).repeat(32)
    a = np.empty((k // 512, 16))
    for p in range(k // 512):
        a[p, :8] = np.random.permutation(np.resize(levels, 8))
        for g in range(8):
            far = levels[np.abs(levels - a[p, g]) >= 10]
            a[p, g + 8] = far[np.random.randint(len(far))]
    return np.exp2(a.ravel()).repeat(32)


BF16 = ml_dtypes.bfloat16


def bf(x):
    return np.asarray(x, np.float32).astype(BF16)


def f64(x):
    return np.asarray(x).astype(np.float64)


M, K1, K2, C, R = 1024, 1536, 512, 1024, 1024
ALPHA = 3.5
DF = 5.0


def setup_inputs():
    s, t = mx_kscale(K1), mx_kscale(K2)
    size = np.exp(0.2 * np.random.standard_normal((M, 1)))
    col = np.concatenate([np.ones(C), np.full(R, ALPHA / np.sqrt(R))]) / np.sqrt(K1 + K2)
    tail = np.random.standard_t(DF, (M, K2)) / np.sqrt(DF / (DF - 2.0))
    return {"x": bf(np.random.standard_normal((M, K1)) * size * s),
            "z": bf(tail * size * t),
            "wx": bf(np.random.standard_normal((K1, C + R)) * col / s[:, None]),
            "wz": bf(np.random.standard_normal((K2, C + R)) * col / t[:, None])}


def reference(x, z, wx, wz):
    regular = mxq(f64(x), 1, "e4m3") @ mxq(f64(wx), 0, "e4m3")
    heavy = mxq(f64(z), 1, "e5m2") @ mxq(f64(wz), 0, "e4m3")
    y = regular + heavy
    logits = y[:, :C]
    resid = y[:, C:]
    virtual = np.sqrt(np.sum(np.square(resid), axis=1, keepdims=True))
    energy = np.log(np.sum(np.exp(logits), axis=1, keepdims=True))
    return logits, resid, virtual - energy

@@ -1,0 +1,300 @@
+from contextlib import ExitStack
+
+import concourse.mybir as mybir
+from concourse.masks import make_identity
+
+M, K1, K2, HEAD, RES = 1024, 1536, 512, 1024, 1024
+N = HEAD + RES
+FLOPS = 2 * M * (K1 + K2) * N
+
+F32 = mybir.dt.float32
+BF16 = mybir.dt.bfloat16
+U32 = mybir.dt.uint32
+U8 = mybir.dt.uint8
+E4M3X4 = mybir.dt.float8_e4m3fn_x4
+E5M2X4 = mybir.dt.float8_e5m2_x4
+ACT = mybir.ActivationFunctionType
+ALU = mybir.AluOpType
+
+P = 128
+PACK = 4
+K_PASS = P * PACK
+PASSES = (K1 + K2) // K_PASS
+TILES = M // P
+PAIRS = TILES // 2
+NB = 512
+HALF = 1024
+
+
+def tile_vim_ood_score_s2_kernel(tc, x, z, wx, wz, logits, resid, score):
+    nc = tc.nc
+
+    x_rows = x.rearrange("(p a) k -> p a k", a=TILES)
+    z_rows = z.rearrange("(p a) k -> p a k", a=TILES)
+    out_rows = [o.rearrange("(p a) n -> p a n", a=TILES) for o in (logits, resid)]
+    score_rows = score.rearrange("(p a) o -> p (a o)", a=TILES)
+
+    def w_rows(c, nb, blocks):
+        src = wx[c * K_PASS:(c + 1) * K_PASS, :] if c < PASSES - 1 else wz
+        return src.rearrange("(p j) n -> p j n", j=PACK)[:, :, nb * NB:(nb + blocks) * NB]
+
+    with ExitStack() as ctx:
+        keep = ctx.enter_context(tc.tile_pool(name="keep", bufs=1))
+        wpool = ctx.enter_context(tc.tile_pool(name="wraw", bufs=6))
+        stage = ctx.enter_context(tc.tile_pool(name="stage", bufs=2))
+        outs = ctx.enter_context(tc.tile_pool(name="outs", bufs=11))
+        psum = ctx.enter_context(tc.psum_pool(name="psum", bufs=1))
+        ctx.enter_context(tc.manual_schedule())
+
+        x_raw = {}
+        z_raw = {}
+        w_raw = {}
+
+        def load_x(pr):
+            t = keep.tile([P, 2, K1], BF16, name=f"x_raw{pr}", align_bytes=64)
+            nc.sync.dma_start(out=t[:], in_=x_rows[:, 2 * pr:2 * pr + 2, :])
+            x_raw[pr] = t
+
+        def load_z(q):
+            t = keep.tile([P, 4, K2], BF16, name=f"z_raw{q}", align_bytes=64)
+            nc.sync.dma_start(out=t[:], in_=z_rows[:, 4 * q:4 * q + 4, :])
+            z_raw[q] = t
+
+        def load_w(c, nb, blocks):
+            t = wpool.tile([P, PACK, blocks * NB], BF16, name=f"w_raw{blocks}", bufs=8 if blocks == 1 else 4, align_bytes=64)
+            nc.sync.dma_start(out=t[:], in_=w_rows(c, nb, blocks))
+            for i in range(blocks):
+                w_raw[c, nb + i] = t[:, :, i * NB:(i + 1) * NB]
+
+        load_x(0)
+        load_z(0)
+        load_x(1)
+        load_x(2)
+        load_z(1)
+        load_x(3)
+        for nb in range(2):
+            for c in range(PASSES):
+                load_w(c, nb, 1)
+        for c in range(PASSES):
+            load_w(c, 2, 2)
+
+        ident = keep.tile([P, P], F32, name="ident")
+        make_identity(nc, ident[:])
+        warm = keep.tile([P, 1], F32, name="warm")
+        nc.vector.memset(warm[:], 1.0)
+        warm_out = keep.tile([P, 1], F32, name="warm_out")
+        nc.scalar.activation(out=warm_out[:], in_=warm[:], func=ACT.Ln)
+
+        x_codes = [keep.tile([P, PASSES, 2 * P], U32, name=f"x_codes{i}", align_bytes=64) for i in range(PAIRS)]
+        x_scales = [keep.tile([P, PASSES, 2 * P], U8, name=f"x_scales{i}", align_bytes=64) for i in range(PAIRS)]
+        w_codes = keep.tile([P, PASSES, N], U32, name="w_codes", align_bytes=64)
+        w_scales = keep.tile([P, PASSES, N], U8, name="w_scales", align_bytes=64)
+        exp_sums = keep.tile([P, TILES], F32, name="exp_sums")
+        sq_sums = keep.tile([P, 2, TILES], F32, name="sq_sums")
+
+        def bank(i, shape):
+            return psum.tile(shape, F32, name=f"bank{i}")
+
+        def words(pr, c, a):
+            if c < PASSES - 1:
+                w = x_raw[pr][:].rearrange("p a k -> p (a k)").bitcast(F32)
+                base = a * (K1 // 2) + c * (K_PASS // 2)
+            else:
+                w = z_raw[pr // 2][:].rearrange("p a k -> p (a k)").bitcast(F32)
+                base = (2 * (pr % 2) + a) * (K2 // 2)
+            return w, base
+
+        t_banks = {}
+        x_grouped = {}
+
+        def transpose_pair(pr):
+            for c in range(PASSES):
+                b = bank(4 * (pr % 2) + c, [P, 2, 2, P])
+                for a in range(2):
+                    w, base = words(pr, c, a)
+                    for u in range(2):
+                        nc.tensor.transpose(b[:, a, u, :], w[:, base + u:base + K_PASS // 2:2], ident[:])
+                t_banks[pr, c] = b
+
+        def empty_t(pr, c, eng):
+            if c % 2 == 0:
+                x_grouped[pr, c // 2] = stage.tile([P, 2, 2 * P * PACK], BF16, name=f"x_grouped{c // 2}", align_bytes=64)
+            dst = x_grouped[pr, c // 2][:, c % 2, :].bitcast(F32).rearrange("p (a r u) -> p a r u", a=2, u=2)
+            src = t_banks[pr, c][:].rearrange("p a u r -> p a r u")
+            if eng == "V":
+                nc.vector.tensor_copy(out=dst, in_=src)
+            else:
+                nc.scalar.copy(out=dst, in_=src)
+
+        def quant_x(pr, c0, c1, fmt):
+            g = x_grouped[pr, c0 // 2]
+            nc.vector.quantize_mx(
+                out=x_codes[pr][:, c0:c1, :].rearrange("p c m -> p (c m)").bitcast(fmt),
+                scales=x_scales[pr][:, c0:c1, :].rearrange("p c m -> p (c m)"),
+                in_=g[:, c0 % 2:c0 % 2 + c1 - c0, :].rearrange("p c q -> p (c q)"),
+            )
+
+        def quant_pair(pr):
+            quant_x(pr, 0, 2, E4M3X4)
+            quant_x(pr, 2, 3, E4M3X4)
+            quant_x(pr, 3, 4, E5M2X4)
+
+        w_grouped = {}
+
+        def interleave_w(c, nb, split):
+            g = stage.tile([P, NB, PACK], BF16, name="w_grouped", bufs=4, align_bytes=64)
+            w_grouped[c, nb] = g
+            src = w_raw[c, nb].rearrange("p j n -> p n j")
+            if split > 0:
+                nc.vector.tensor_copy(out=g[:, 0:split, :], in_=src[:, 0:split, :])
+            if split < NB:
+                nc.scalar.copy(out=g[:, split:NB, :], in_=src[:, split:NB, :])
+
+        def quant_w(c, nb):
+            cols = slice(nb * NB, (nb + 1) * NB)
+            nc.vector.quantize_mx(
+                out=w_codes[:, c, cols].bitcast(E4M3X4),
+                scales=w_scales[:, c, cols],
+                in_=w_grouped[c, nb][:].rearrange("p n j -> p (n j)"),
+            )
+
+        acc = {}
+
+        def product(a, nb, c):
+            if c == 0:
+                acc[a, nb] = bank(a, [P, NB])
+            rows = slice((a % 2) * P, (a % 2 + 1) * P)
+            cols = slice(nb * NB, (nb + 1) * NB)
+            nc.tensor.matmul_mx(
+                out=acc[a, nb][:],
+                lhsT=x_codes[a // 2][:, c, rows].bitcast(E4M3X4 if c < PASSES - 1 else E5M2X4),
+                lhsT_scale=x_scales[a // 2][:, c, rows],
+                rhs=w_codes[:, c, cols].bitcast(E4M3X4),
+                rhs_scale=w_scales[:, c, cols],
+                start=(c == 0),
+                stop=(c == PASSES - 1),
+            )
+
+        y = {}
+
+        def empty_acc(a, nb, eng):
+            if nb % 2 == 0:
+                y[a, nb // 2] = outs.tile([P, HALF], F32, name="y")
+            dst = y[a, nb // 2][:, (nb % 2) * NB:(nb % 2 + 1) * NB]
+            if eng == "V":
+                nc.vector.tensor_copy(out=dst, in_=acc[a, nb][:])
+            else:
+                nc.scalar.copy(out=dst, in_=acc[a, nb][:])
+
+        def store(a, h, lo, hi):
+            nc.sync.dma_start(out=out_rows[h][:, a, lo:hi], in_=y[a, h][:, lo:hi])
+
+        def exp_row(a):
+            junk = stage.tile([P, HALF], BF16, name="junk_s")
+            nc.scalar.activation(out=junk[:], in_=y[a, 0][:], func=ACT.Exp, accum_out=exp_sums[:, a:a + 1])
+
+        def square_row(a, i, eng):
+            src = y[a, 1][:, i * NB:(i + 1) * NB]
+            acc_out = sq_sums[:, i, a:a + 1]
+            if eng == "V":
+                junk = stage.tile([P, NB], BF16, name="junk_v")
+                nc.vector.scalar_tensor_tensor(out=junk[:], in0=src, scalar=1.0, in1=src, op0=ALU.mult, op1=ALU.mult, accum_out=acc_out)
+            else:
+                junk = stage.tile([P, HALF], BF16, name="junk_s")
+                nc.scalar.activation(out=junk[:, 0:NB], in_=src, func=ACT.Square, accum_out=acc_out)
+
+        for pr in range(PAIRS):
+            transpose_pair(pr)
+            empty_t(pr, 0, "V")
+            if pr == PAIRS - 1:
+                interleave_w(0, 0, 256)
+            empty_t(pr, 1, "S")
+            empty_t(pr, 2, "S")
+            empty_t(pr, 3, "S")
+            if pr == PAIRS - 1:
+                quant_w(0, 0)
+            quant_pair(pr)
+        for c in range(PASSES):
+            if c + 1 < PASSES:
+                interleave_w(c + 1, 0, 256)
+                quant_w(c + 1, 0)
+            else:
+                interleave_w(0, 1, 256)
+            for a in range(TILES):
+                product(a, 0, c)
+        for c in range(1, PASSES):
+            interleave_w(c, 1, 256)
+            quant_w(c - 1, 1)
+            if c >= 2:
+                for a in range(2 * c - 4, 2 * c - 2):
+                    empty_acc(a, 0, "V" if a % 2 == 0 else "S")
+        interleave_w(0, 2, 256)
+        quant_w(3, 1)
+        for a in range(4, TILES):
+            empty_acc(a, 0, "V" if a % 2 == 0 else "S")
+        for c in range(PASSES):
+            for a in range(4):
+                product(a, 1, c)
+        chain = [(c, nb) for nb in (2, 3) for c in range(PASSES)]
+        work = []
+        for i in range(len(chain)):
+            if i + 1 < len(chain):
+                work.append((interleave_w, chain[i + 1]))
+            work.append((quant_w, chain[i]))
+
+        def weave():
+            if work:
+                f, args = work.pop(0)
+                if f is interleave_w:
+                    f(*args, 256 if args in ((1, 2),(2,2)) else 512)
+                else:
+                    f(*args)
+
+        for a in range(TILES):
+            if a >= 4:
+                for c in range(PASSES):
+                    product(a, 1, c)
+            weave()
+            empty_acc(a, 1, "S")
+            store(a, 0, 0, HALF)
+            if a >= 4:
+                exp_row(a - 4)
+        for c in range(PASSES):
+            for a in range(4):
+                product(a, 2, c)
+        for a in range(TILES):
+            if a >= 4:
+                for c in range(PASSES):
+                    product(a, 2, c)
+            weave()
+            if a % 2 == 1:
+                weave()
+            empty_acc(a, 2, "V" if a in (1, 3, 5, 7) else "S")
+            store(a, 1, 0, NB)
+            if a % 2 == 1:
+                exp_row(4 + a // 2)
+        for a in range(3):
+            square_row(a, 0, "V")
+
+        energy = keep.tile([P, TILES], F32, name="energy")
+        virtual = keep.tile([P, TILES], F32, name="virtual")
+        total = keep.tile([P, TILES], F32, name="total")
+        result = keep.tile([P, TILES], F32, name="result")
+        nc.scalar.activation(out=energy[:], in_=exp_sums[:], func=ACT.Ln)
+        nc.scalar.activation(out=warm_out[:], in_=warm[:], func=ACT.Sqrt)
+
+        for a in range(TILES):
+            for c in range(PASSES):
+                product(a, 3, c)
+            if a >= 3:
+                square_row(a, 0, "S")
+            empty_acc(a, 3, "V")
+            store(a, 1, NB, HALF)
+            if a > 0:
+                square_row(a - 1, 1, "V" if a % 2 == 0 else "S")
+        square_row(TILES - 1, 1, "S")
+
+        nc.vector.tensor_add(out=total[:], in0=sq_sums[:, 0, :], in1=sq_sums[:, 1, :])
+        nc.scalar.activation(out=virtual[:], in_=total[:], func=ACT.Sqrt)
+        nc.vector.tensor_sub(out=result[:], in0=virtual[:], in1=energy[:])
+        nc.sync.dma_start(out=score_rows, in_=result[:])

@@ -42,7 +42,7 @@ def tile_vim_ood_score_s2_kernel(tc, x, z, wx, wz, logits, resid, score):
         keep = ctx.enter_context(tc.tile_pool(name="keep", bufs=1))
         wpool = ctx.enter_context(tc.tile_pool(name="wraw", bufs=6))
         stage = ctx.enter_context(tc.tile_pool(name="stage", bufs=2))
-        outs = ctx.enter_context(tc.tile_pool(name="outs", bufs=11))
+        outs = ctx.enter_context(tc.tile_pool(name="outs", bufs=10))
         psum = ctx.enter_context(tc.psum_pool(name="psum", bufs=1))
         ctx.enter_context(tc.manual_schedule())
 
@@ -83,7 +83,7 @@ def tile_vim_ood_score_s2_kernel(tc, x, z, wx, wz, logits, resid, score):
         warm = keep.tile([P, 1], F32, name="warm")
         nc.vector.memset(warm[:], 1.0)
         warm_out = keep.tile([P, 1], F32, name="warm_out")
-        nc.scalar.activation(out=warm_out[:], in_=warm[:], func=ACT.Ln)
+        nc.scalar.activation(out=warm_out[:], in_=warm[:], func=ACT.Exp)
 
         x_codes = [keep.tile([P, PASSES, 2 * P], U32, name=f"x_codes{i}", align_bytes=64) for i in range(PAIRS)]
         x_scales = [keep.tile([P, PASSES, 2 * P], U8, name=f"x_scales{i}", align_bytes=64) for i in range(PAIRS)]
@@ -107,9 +107,19 @@ def tile_vim_ood_score_s2_kernel(tc, x, z, wx, wz, logits, resid, score):
         t_banks = {}
         x_grouped = {}
 
+        zeros = keep.tile([P, NB], BF16, name="zeros")
+        nc.vector.memset(zeros[:], 0.0)
+
+        def keep_warm(b):
+            nc.tensor.matmul(b[:].rearrange("p a u r -> p (a u r)"), lhsT=zeros[:, 0:P], rhs=zeros[:], start=True, stop=True)
+
+        WARM = ((9, 0, 2, 0), (2, 0, 2, 0), (2, 0, 2, 0), (2, 0, 2, 0))
+
         def transpose_pair(pr):
             for c in range(PASSES):
                 b = bank(4 * (pr % 2) + c, [P, 2, 2, P])
+                for i in range(WARM[pr][c]):
+                    keep_warm(b)
                 for a in range(2):
                     w, base = words(pr, c, a)
                     for u in range(2):

@@ -66,15 +66,17 @@ def tile_vim_ood_score_s2_kernel(tc, x, z, wx, wz, logits, resid, score):
             for i in range(blocks):
                 w_raw[c, nb + i] = t[:, :, i * NB:(i + 1) * NB]
 
+        load_w(0, 0, 1)
         load_x(0)
         load_z(0)
         load_x(1)
         load_x(2)
         load_z(1)
         load_x(3)
-        for nb in range(2):
-            for c in range(PASSES):
-                load_w(c, nb, 1)
+        for c in range(1, PASSES):
+            load_w(c, 0, 1)
+        for c in range(PASSES):
+            load_w(c, 1, 1)
         for c in range(PASSES):
             load_w(c, 2, 2)
 
@@ -82,6 +84,8 @@ def tile_vim_ood_score_s2_kernel(tc, x, z, wx, wz, logits, resid, score):
         make_identity(nc, ident[:])
         warm = keep.tile([P, 1], F32, name="warm")
         nc.vector.memset(warm[:], 1.0)
+        halves = keep.tile([P, TILES], F32, name="halves")
+        nc.gpsimd.memset(halves[:], 0.5)
         warm_out = keep.tile([P, 1], F32, name="warm_out")
         nc.scalar.activation(out=warm_out[:], in_=warm[:], func=ACT.Exp)
 
@@ -90,7 +94,7 @@ def tile_vim_ood_score_s2_kernel(tc, x, z, wx, wz, logits, resid, score):
         w_codes = keep.tile([P, PASSES, N], U32, name="w_codes", align_bytes=64)
         w_scales = keep.tile([P, PASSES, N], U8, name="w_scales", align_bytes=64)
         exp_sums = keep.tile([P, TILES], F32, name="exp_sums")
-        sq_sums = keep.tile([P, 2, TILES], F32, name="sq_sums")
+        sq_sums = keep.tile([P, 3, TILES], F32, name="sq_sums")
 
         def bank(i, shape):
             return psum.tile(shape, F32, name=f"bank{i}")
@@ -104,22 +108,13 @@ def tile_vim_ood_score_s2_kernel(tc, x, z, wx, wz, logits, resid, score):
                 base = (2 * (pr % 2) + a) * (K2 // 2)
             return w, base
 
+        T_ORDER = ((0, 1, 2, 3), (3, 0, 1, 2))
         t_banks = {}
         x_grouped = {}
 
-        zeros = keep.tile([P, NB], BF16, name="zeros")
-        nc.vector.memset(zeros[:], 0.0)
-
-        def keep_warm(b):
-            nc.tensor.matmul(b[:].rearrange("p a u r -> p (a u r)"), lhsT=zeros[:, 0:P], rhs=zeros[:], start=True, stop=True)
-
-        WARM = ((9, 0, 2, 0), (2, 0, 2, 0), (2, 0, 2, 0), (2, 0, 2, 0))
-
         def transpose_pair(pr):
-            for c in range(PASSES):
-                b = bank(4 * (pr % 2) + c, [P, 2, 2, P])
-                for i in range(WARM[pr][c]):
-                    keep_warm(b)
+            for i, c in enumerate(T_ORDER[pr % 2]):
+                b = bank(i, [P, 2, 2, P])
                 for a in range(2):
                     w, base = words(pr, c, a)
                     for u in range(2):
@@ -127,7 +122,7 @@ def tile_vim_ood_score_s2_kernel(tc, x, z, wx, wz, logits, resid, score):
                 t_banks[pr, c] = b
 
         def empty_t(pr, c, eng):
-            if c % 2 == 0:
+            if (pr, c // 2) not in x_grouped:
                 x_grouped[pr, c // 2] = stage.tile([P, 2, 2 * P * PACK], BF16, name=f"x_grouped{c // 2}", align_bytes=64)
             dst = x_grouped[pr, c // 2][:, c % 2, :].bitcast(F32).rearrange("p (a r u) -> p a r u", a=2, u=2)
             src = t_banks[pr, c][:].rearrange("p a u r -> p a r u")
@@ -154,11 +149,13 @@ def tile_vim_ood_score_s2_kernel(tc, x, z, wx, wz, logits, resid, score):
         def interleave_w(c, nb, split):
             g = stage.tile([P, NB, PACK], BF16, name="w_grouped", bufs=4, align_bytes=64)
             w_grouped[c, nb] = g
-            src = w_raw[c, nb].rearrange("p j n -> p n j")
+            src = w_raw[c, nb].rearrange("p j (n i) -> p n j i", i=4)
+            dst = g[:].rearrange("p (n i) j -> p n j i", i=4)
+            cut = split // 4
             if split > 0:
-                nc.vector.tensor_copy(out=g[:, 0:split, :], in_=src[:, 0:split, :])
+                nc.vector.tensor_copy(out=dst[:, 0:cut], in_=src[:, 0:cut])
             if split < NB:
-                nc.scalar.copy(out=g[:, split:NB, :], in_=src[:, split:NB, :])
+                nc.scalar.copy(out=dst[:, cut:], in_=src[:, cut:])
 
         def quant_w(c, nb):
             cols = slice(nb * NB, (nb + 1) * NB)
@@ -172,7 +169,7 @@ def tile_vim_ood_score_s2_kernel(tc, x, z, wx, wz, logits, resid, score):
 
         def product(a, nb, c):
             if c == 0:
-                acc[a, nb] = bank(a, [P, NB])
+                acc[a, nb] = bank((a + 4) % 8, [P, NB])
             rows = slice((a % 2) * P, (a % 2 + 1) * P)
             cols = slice(nb * NB, (nb + 1) * NB)
             nc.tensor.matmul_mx(
@@ -190,11 +187,13 @@ def tile_vim_ood_score_s2_kernel(tc, x, z, wx, wz, logits, resid, score):
         def empty_acc(a, nb, eng):
             if nb % 2 == 0:
                 y[a, nb // 2] = outs.tile([P, HALF], F32, name="y")
-            dst = y[a, nb // 2][:, (nb % 2) * NB:(nb % 2 + 1) * NB]
+            copy_cols(eng, y[a, nb // 2][:, (nb % 2) * NB:(nb % 2 + 1) * NB], acc[a, nb][:])
+
+        def copy_cols(eng, dst, src):
             if eng == "V":
-                nc.vector.tensor_copy(out=dst, in_=acc[a, nb][:])
+                nc.vector.tensor_copy(out=dst, in_=src)
             else:
-                nc.scalar.copy(out=dst, in_=acc[a, nb][:])
+                nc.scalar.copy(out=dst, in_=src)
 
         def store(a, h, lo, hi):
             nc.sync.dma_start(out=out_rows[h][:, a, lo:hi], in_=y[a, h][:, lo:hi])
@@ -204,107 +203,116 @@ def tile_vim_ood_score_s2_kernel(tc, x, z, wx, wz, logits, resid, score):
             nc.scalar.activation(out=junk[:], in_=y[a, 0][:], func=ACT.Exp, accum_out=exp_sums[:, a:a + 1])
 
         def square_row(a, i, eng):
-            src = y[a, 1][:, i * NB:(i + 1) * NB]
-            acc_out = sq_sums[:, i, a:a + 1]
+            square_cols(eng, y[a, 1][:, i * NB:(i + 1) * NB], sq_sums[:, i, a:a + 1])
+
+        def square_cols(eng, src, sums):
+            width = src.shape[1]
             if eng == "V":
                 junk = stage.tile([P, NB], BF16, name="junk_v")
-                nc.vector.scalar_tensor_tensor(out=junk[:], in0=src, scalar=1.0, in1=src, op0=ALU.mult, op1=ALU.mult, accum_out=acc_out)
+                nc.vector.scalar_tensor_tensor(out=junk[:, 0:width], in0=src, scalar=1.0, in1=src, op0=ALU.mult, op1=ALU.mult, accum_out=sums)
             else:
                 junk = stage.tile([P, HALF], BF16, name="junk_s")
-                nc.scalar.activation(out=junk[:, 0:NB], in_=src, func=ACT.Square, accum_out=acc_out)
+                nc.scalar.activation(out=junk[:, 0:width], in_=src, func=ACT.Square, accum_out=sums)
 
+        def mx(nb, tiles, cs=range(PASSES)):
+            for c in cs:
+                for a in tiles:
+                    product(a, nb, c)
+
+        interleave_w(0, 0, 512)
+        quant_w(0, 0)
         for pr in range(PAIRS):
             transpose_pair(pr)
-            empty_t(pr, 0, "V")
+            c0, c1, c2, c3 = T_ORDER[pr % 2]
+            if pr >= 2:
+                mx(0, (2 * pr - 4, 2 * pr - 3), (0,))
+            empty_t(pr, c0, "S")
+            empty_t(pr, c1, "V")
+            empty_t(pr, c2, "S")
+            empty_t(pr, c3, "S")
             if pr == PAIRS - 1:
-                interleave_w(0, 0, 256)
-            empty_t(pr, 1, "S")
-            empty_t(pr, 2, "S")
-            empty_t(pr, 3, "S")
-            if pr == PAIRS - 1:
-                quant_w(0, 0)
+                interleave_w(1, 0, 384)
             quant_pair(pr)
-        for c in range(PASSES):
-            if c + 1 < PASSES:
-                interleave_w(c + 1, 0, 256)
-                quant_w(c + 1, 0)
-            else:
-                interleave_w(0, 1, 256)
-            for a in range(TILES):
-                product(a, 0, c)
-        for c in range(1, PASSES):
-            interleave_w(c, 1, 256)
-            quant_w(c - 1, 1)
-            if c >= 2:
-                for a in range(2 * c - 4, 2 * c - 2):
-                    empty_acc(a, 0, "V" if a % 2 == 0 else "S")
-        interleave_w(0, 2, 256)
+        quant_w(1, 0)
+        mx(0, (4, 5, 6, 7), (0,))
+        mx(0, range(TILES), (1,))
+        interleave_w(2, 0, 256)
+        interleave_w(3, 0, 256)
+        quant_w(2, 0)
+        mx(0, range(TILES), (2,))
+        interleave_w(0, 1, 256)
+        quant_w(3, 0)
+        mx(0, range(TILES), (3,))
+        interleave_w(1, 1, 256)
+        quant_w(0, 1)
+        interleave_w(2, 1, 256)
+        quant_w(1, 1)
+        interleave_w(3, 1, 256)
+        empty_acc(0, 0, "S")
+        empty_acc(1, 0, "V")
+        quant_w(2, 1)
+        empty_acc(2, 0, "S")
+        empty_acc(3, 0, "V")
         quant_w(3, 1)
+        chain = [(0, 2), (0, 3), (1, 2), (2, 2), (3, 2), (1, 3), (2, 3), (3, 3)]
         for a in range(4, TILES):
-            empty_acc(a, 0, "V" if a % 2 == 0 else "S")
-        for c in range(PASSES):
-            for a in range(4):
-                product(a, 1, c)
-        chain = [(c, nb) for nb in (2, 3) for c in range(PASSES)]
-        work = []
-        for i in range(len(chain)):
-            if i + 1 < len(chain):
-                work.append((interleave_w, chain[i + 1]))
-            work.append((quant_w, chain[i]))
-
-        def weave():
-            if work:
-                f, args = work.pop(0)
-                if f is interleave_w:
-                    f(*args, 256 if args in ((1, 2),(2,2)) else 512)
-                else:
-                    f(*args)
-
+            empty_acc(a, 0, "S")
+        interleave_w(*chain[0], 512)
+        mx(1, range(4))
+        for i in range(8):
+            if i + 1 < 8:
+                interleave_w(*chain[i + 1], 512)
+            quant_w(*chain[i])
         for a in range(TILES):
             if a >= 4:
-                for c in range(PASSES):
-                    product(a, 1, c)
-            weave()
+                mx(1, (a,))
             empty_acc(a, 1, "S")
             store(a, 0, 0, HALF)
-            if a >= 4:
-                exp_row(a - 4)
-        for c in range(PASSES):
-            for a in range(4):
-                product(a, 2, c)
+            if a % 2 == 1:
+                exp_row(a - 1)
+                exp_row(a)
+        mx(2, range(4))
         for a in range(TILES):
             if a >= 4:
-                for c in range(PASSES):
-                    product(a, 2, c)
-            weave()
-            if a % 2 == 1:
-                weave()
-            empty_acc(a, 2, "V" if a in (1, 3, 5, 7) else "S")
+                mx(2, (a,))
+            empty_acc(a, 2, "S" if a < 4 else "V")
             store(a, 1, 0, NB)
-            if a % 2 == 1:
-                exp_row(4 + a // 2)
-        for a in range(3):
-            square_row(a, 0, "V")
 
         energy = keep.tile([P, TILES], F32, name="energy")
         virtual = keep.tile([P, TILES], F32, name="virtual")
         total = keep.tile([P, TILES], F32, name="total")
         result = keep.tile([P, TILES], F32, name="result")
         nc.scalar.activation(out=energy[:], in_=exp_sums[:], func=ACT.Ln)
-        nc.scalar.activation(out=warm_out[:], in_=warm[:], func=ACT.Sqrt)
 
-        for a in range(TILES):
-            for c in range(PASSES):
-                product(a, 3, c)
-            if a >= 3:
-                square_row(a, 0, "S")
-            empty_acc(a, 3, "V")
+        def finish(lo, hi):
+            cols = slice(lo, hi)
+            if hi == TILES:
+                nc.vector.scalar_tensor_tensor(out=total[:, cols], in0=sq_sums[:, 0, cols], scalar=sq_sums[:, 2, cols], in1=sq_sums[:, 1, cols], op0=ALU.add, op1=ALU.add)
+            else:
+                nc.vector.tensor_add(out=total[:, cols], in0=sq_sums[:, 0, cols], in1=sq_sums[:, 1, cols])
+            nc.gpsimd.tensor_tensor(out=virtual[:, cols], in0=total[:, cols], in1=halves[:, cols], op=ALU.pow)
+            nc.gpsimd.tensor_tensor(out=result[:, cols], in0=virtual[:, cols], in1=energy[:, cols], op=ALU.subtract)
+
+        for a in range(TILES - 1):
+            mx(3, (a,))
+            mine, other = ("V", "S") if a % 2 == 0 else ("S", "V")
+            square_row(a, 0, other)
+            empty_acc(a, 3, mine)
             store(a, 1, NB, HALF)
             if a > 0:
-                square_row(a - 1, 1, "V" if a % 2 == 0 else "S")
-        square_row(TILES - 1, 1, "S")
-
-        nc.vector.tensor_add(out=total[:], in0=sq_sums[:, 0, :], in1=sq_sums[:, 1, :])
-        nc.scalar.activation(out=virtual[:], in_=total[:], func=ACT.Sqrt)
-        nc.vector.tensor_sub(out=result[:], in0=virtual[:], in1=energy[:])
+                square_row(a - 1, 1, mine)
+            if a >= 5:
+                finish(4 * (a - 5), 2 * a - 6)
+        last = TILES - 1
+        mx(3, (last,))
+        square_row(last, 0, "V")
+        square_row(last - 1, 1, "S")
+        finish(last - 1, last)
+        src = acc[last, 3]
+        for eng, lo, hi in (("V", 0, NB // 2), ("S", NB // 2, NB)):
+            copy_cols(eng, y[last, 1][:, NB + lo:NB + hi], src[:, lo:hi])
+            store(last, 1, NB + lo, NB + hi)
+        square_cols("V", y[last, 1][:, NB:NB + NB // 2], sq_sums[:, 2, last:last + 1])
+        square_cols("S", y[last, 1][:, NB + NB // 2:HALF], sq_sums[:, 1, last:last + 1])
+        finish(last, TILES)
         nc.sync.dma_start(out=score_rows, in_=result[:])

@@ -3,8 +3,10 @@ from contextlib import ExitStack
 import concourse.mybir as mybir
 from concourse.masks import make_identity
 
-M, K1, K2, HEAD, RES = 1024, 1536, 512, 1024, 1024
-N = HEAD + RES
+M = 1024
+K1, K2 = 1536, 512
+HALF = 1024
+N = 2 * HALF
 FLOPS = 2 * M * (K1 + K2) * N
 
 F32 = mybir.dt.float32
@@ -20,10 +22,11 @@ P = 128
 PACK = 4
 K_PASS = P * PACK
 PASSES = (K1 + K2) // K_PASS
+Z_PASS = PASSES - 1
 TILES = M // P
 PAIRS = TILES // 2
-NB = 512
-HALF = 1024
+BLOCK = 512
+VECTOR, SCALAR = "vector", "scalar"
 
 
 def tile_vim_ood_score_s2_kernel(tc, x, z, wx, wz, logits, resid, score):
@@ -31,47 +34,45 @@ def tile_vim_ood_score_s2_kernel(tc, x, z, wx, wz, logits, resid, score):
 
     x_rows = x.rearrange("(p a) k -> p a k", a=TILES)
     z_rows = z.rearrange("(p a) k -> p a k", a=TILES)
-    out_rows = [o.rearrange("(p a) n -> p a n", a=TILES) for o in (logits, resid)]
+    out_rows = [y.rearrange("(p a) n -> p a n", a=TILES) for y in (logits, resid)]
     score_rows = score.rearrange("(p a) o -> p (a o)", a=TILES)
-
-    def w_rows(c, nb, blocks):
-        src = wx[c * K_PASS:(c + 1) * K_PASS, :] if c < PASSES - 1 else wz
-        return src.rearrange("(p j) n -> p j n", j=PACK)[:, :, nb * NB:(nb + blocks) * NB]
 
     with ExitStack() as ctx:
         keep = ctx.enter_context(tc.tile_pool(name="keep", bufs=1))
-        wpool = ctx.enter_context(tc.tile_pool(name="wraw", bufs=6))
+        w_pool = ctx.enter_context(tc.tile_pool(name="w_pool", bufs=1))
         stage = ctx.enter_context(tc.tile_pool(name="stage", bufs=2))
-        outs = ctx.enter_context(tc.tile_pool(name="outs", bufs=10))
+        y_pool = ctx.enter_context(tc.tile_pool(name="y_pool", bufs=10))
         psum = ctx.enter_context(tc.psum_pool(name="psum", bufs=1))
         ctx.enter_context(tc.manual_schedule())
 
-        x_raw = {}
-        z_raw = {}
-        w_raw = {}
+        x_raw, z_raw, w_raw = {}, {}, {}
 
-        def load_x(pr):
-            t = keep.tile([P, 2, K1], BF16, name=f"x_raw{pr}", align_bytes=64)
-            nc.sync.dma_start(out=t[:], in_=x_rows[:, 2 * pr:2 * pr + 2, :])
-            x_raw[pr] = t
+        def load_x(pair):
+            raw = keep.tile([P, 2, K1], BF16, name=f"x_raw{pair}", align_bytes=64)
+            nc.sync.dma_start(out=raw[:], in_=x_rows[:, 2 * pair : 2 * pair + 2, :])
+            x_raw[pair] = raw
 
-        def load_z(q):
-            t = keep.tile([P, 4, K2], BF16, name=f"z_raw{q}", align_bytes=64)
-            nc.sync.dma_start(out=t[:], in_=z_rows[:, 4 * q:4 * q + 4, :])
-            z_raw[q] = t
+        def load_z(pair):
+            raw = keep.tile([P, 4, K2], BF16, name=f"z_raw{pair}", align_bytes=64)
+            nc.sync.dma_start(out=raw[:], in_=z_rows[:, 2 * pair : 2 * pair + 4, :])
+            z_raw[pair], z_raw[pair + 1] = raw[:, 0:2, :], raw[:, 2:4, :]
 
-        def load_w(c, nb, blocks):
-            t = wpool.tile([P, PACK, blocks * NB], BF16, name=f"w_raw{blocks}", bufs=8 if blocks == 1 else 4, align_bytes=64)
-            nc.sync.dma_start(out=t[:], in_=w_rows(c, nb, blocks))
+        def load_w(c, block, blocks):
+            rows = wz if c == Z_PASS else wx[c * K_PASS : (c + 1) * K_PASS, :]
+            cols = slice(block * BLOCK, (block + blocks) * BLOCK)
+            raw = w_pool.tile(
+                [P, PACK, blocks * BLOCK], BF16, name=f"w_raw{blocks}", bufs=8 // blocks, align_bytes=64
+            )
+            nc.sync.dma_start(out=raw[:], in_=rows.rearrange("(p j) n -> p j n", j=PACK)[:, :, cols])
             for i in range(blocks):
-                w_raw[c, nb + i] = t[:, :, i * NB:(i + 1) * NB]
+                w_raw[c, block + i] = raw[:, :, i * BLOCK : (i + 1) * BLOCK]
 
         load_w(0, 0, 1)
         load_x(0)
         load_z(0)
         load_x(1)
         load_x(2)
-        load_z(1)
+        load_z(2)
         load_x(3)
         for c in range(1, PASSES):
             load_w(c, 0, 1)
@@ -80,239 +81,233 @@ def tile_vim_ood_score_s2_kernel(tc, x, z, wx, wz, logits, resid, score):
         for c in range(PASSES):
             load_w(c, 2, 2)
 
-        ident = keep.tile([P, P], F32, name="ident")
-        make_identity(nc, ident[:])
-        warm = keep.tile([P, 1], F32, name="warm")
-        nc.vector.memset(warm[:], 1.0)
-        halves = keep.tile([P, TILES], F32, name="halves")
-        nc.gpsimd.memset(halves[:], 0.5)
-        warm_out = keep.tile([P, 1], F32, name="warm_out")
-        nc.scalar.activation(out=warm_out[:], in_=warm[:], func=ACT.Exp)
+        identity = keep.tile([P, P], F32, name="identity")
+        make_identity(nc, identity[:])
+        one = keep.tile([P, 1], F32, name="one")
+        nc.vector.memset(one[:], 1.0)
+        unused = keep.tile([P, 1], F32, name="unused")
+        nc.scalar.activation(out=unused[:], in_=one[:], func=ACT.Exp)
 
         x_codes = [keep.tile([P, PASSES, 2 * P], U32, name=f"x_codes{i}", align_bytes=64) for i in range(PAIRS)]
         x_scales = [keep.tile([P, PASSES, 2 * P], U8, name=f"x_scales{i}", align_bytes=64) for i in range(PAIRS)]
         w_codes = keep.tile([P, PASSES, N], U32, name="w_codes", align_bytes=64)
         w_scales = keep.tile([P, PASSES, N], U8, name="w_scales", align_bytes=64)
         exp_sums = keep.tile([P, TILES], F32, name="exp_sums")
-        sq_sums = keep.tile([P, 3, TILES], F32, name="sq_sums")
+        square_sums = keep.tile([P, 2, TILES], F32, name="square_sums")
 
         def bank(i, shape):
             return psum.tile(shape, F32, name=f"bank{i}")
 
-        def words(pr, c, a):
-            if c < PASSES - 1:
-                w = x_raw[pr][:].rearrange("p a k -> p (a k)").bitcast(F32)
-                base = a * (K1 // 2) + c * (K_PASS // 2)
+        def copy(engine, out, in_):
+            if engine == VECTOR:
+                nc.vector.tensor_copy(out=out, in_=in_)
             else:
-                w = z_raw[pr // 2][:].rearrange("p a k -> p (a k)").bitcast(F32)
-                base = (2 * (pr % 2) + a) * (K2 // 2)
-            return w, base
+                nc.scalar.copy(out=out, in_=in_)
 
-        T_ORDER = ((0, 1, 2, 3), (3, 0, 1, 2))
-        t_banks = {}
-        x_grouped = {}
+        transposed, x_grouped = {}, {}
 
-        def transpose_pair(pr):
-            for i, c in enumerate(T_ORDER[pr % 2]):
-                b = bank(i, [P, 2, 2, P])
+        def pass_order(pair):
+            return (0, 1, 2, Z_PASS) if pair % 2 == 0 else (Z_PASS, 0, 1, 2)
+
+        def transpose_pair(pair):
+            for i, c in enumerate(pass_order(pair)):
+                out = bank(i, [P, 2, 2, P])
+                raw, first_k = (z_raw[pair], 0) if c == Z_PASS else (x_raw[pair], c * K_PASS)
                 for a in range(2):
-                    w, base = words(pr, c, a)
+                    words = raw[:, a, first_k : first_k + K_PASS].bitcast(F32)
                     for u in range(2):
-                        nc.tensor.transpose(b[:, a, u, :], w[:, base + u:base + K_PASS // 2:2], ident[:])
-                t_banks[pr, c] = b
+                        nc.tensor.transpose(out[:, a, u, :], words[:, u::2], identity[:])
+                transposed[pair, c] = out
 
-        def empty_t(pr, c, eng):
-            if (pr, c // 2) not in x_grouped:
-                x_grouped[pr, c // 2] = stage.tile([P, 2, 2 * P * PACK], BF16, name=f"x_grouped{c // 2}", align_bytes=64)
-            dst = x_grouped[pr, c // 2][:, c % 2, :].bitcast(F32).rearrange("p (a r u) -> p a r u", a=2, u=2)
-            src = t_banks[pr, c][:].rearrange("p a u r -> p a r u")
-            if eng == "V":
-                nc.vector.tensor_copy(out=dst, in_=src)
-            else:
-                nc.scalar.copy(out=dst, in_=src)
-
-        def quant_x(pr, c0, c1, fmt):
-            g = x_grouped[pr, c0 // 2]
-            nc.vector.quantize_mx(
-                out=x_codes[pr][:, c0:c1, :].rearrange("p c m -> p (c m)").bitcast(fmt),
-                scales=x_scales[pr][:, c0:c1, :].rearrange("p c m -> p (c m)"),
-                in_=g[:, c0 % 2:c0 % 2 + c1 - c0, :].rearrange("p c q -> p (c q)"),
+        def group_x(pair, c, engine):
+            half = c // 2
+            if (pair, half) not in x_grouped:
+                grouped = stage.tile([P, 2, 2 * P * PACK], BF16, name=f"x_grouped{half}", align_bytes=64)
+                x_grouped[pair, half] = grouped
+            words = x_grouped[pair, half][:, c % 2, :].bitcast(F32)
+            copy(
+                engine,
+                out=words.rearrange("p (a m u) -> p a m u", a=2, u=2),
+                in_=transposed[pair, c][:].rearrange("p a u m -> p a m u"),
             )
 
-        def quant_pair(pr):
-            quant_x(pr, 0, 2, E4M3X4)
-            quant_x(pr, 2, 3, E4M3X4)
-            quant_x(pr, 3, 4, E5M2X4)
+        def quantise_x(pair):
+            for first, end, fmt in ((0, 2, E4M3X4), (2, Z_PASS, E4M3X4), (Z_PASS, PASSES, E5M2X4)):
+                grouped = x_grouped[pair, first // 2][:, first % 2 : first % 2 + end - first, :]
+                nc.vector.quantize_mx(
+                    out=x_codes[pair][:, first:end, :].rearrange("p c m -> p (c m)").bitcast(fmt),
+                    scales=x_scales[pair][:, first:end, :].rearrange("p c m -> p (c m)"),
+                    in_=grouped.rearrange("p c q -> p (c q)"),
+                )
 
         w_grouped = {}
 
-        def interleave_w(c, nb, split):
-            g = stage.tile([P, NB, PACK], BF16, name="w_grouped", bufs=4, align_bytes=64)
-            w_grouped[c, nb] = g
-            src = w_raw[c, nb].rearrange("p j (n i) -> p n j i", i=4)
-            dst = g[:].rearrange("p (n i) j -> p n j i", i=4)
-            cut = split // 4
-            if split > 0:
-                nc.vector.tensor_copy(out=dst[:, 0:cut], in_=src[:, 0:cut])
-            if split < NB:
-                nc.scalar.copy(out=dst[:, cut:], in_=src[:, cut:])
+        def group_w(c, block, vector_cols):
+            grouped = stage.tile([P, BLOCK, PACK], BF16, name="w_grouped", bufs=4, align_bytes=64)
+            w_grouped[c, block] = grouped
+            src = w_raw[c, block].rearrange("p j (n i) -> p n j i", i=4)
+            dst = grouped[:].rearrange("p (n i) j -> p n j i", i=4)
+            cut = vector_cols // 4
+            copy(VECTOR, dst[:, 0:cut], src[:, 0:cut])
+            if vector_cols < BLOCK:
+                copy(SCALAR, dst[:, cut:], src[:, cut:])
 
-        def quant_w(c, nb):
-            cols = slice(nb * NB, (nb + 1) * NB)
+        def quantise_w(c, block):
+            cols = slice(block * BLOCK, (block + 1) * BLOCK)
             nc.vector.quantize_mx(
                 out=w_codes[:, c, cols].bitcast(E4M3X4),
                 scales=w_scales[:, c, cols],
-                in_=w_grouped[c, nb][:].rearrange("p n j -> p (n j)"),
+                in_=w_grouped[c, block][:].rearrange("p n j -> p (n j)"),
             )
 
-        acc = {}
+        sums, y = {}, {}
 
-        def product(a, nb, c):
-            if c == 0:
-                acc[a, nb] = bank((a + 4) % 8, [P, NB])
-            rows = slice((a % 2) * P, (a % 2 + 1) * P)
-            cols = slice(nb * NB, (nb + 1) * NB)
-            nc.tensor.matmul_mx(
-                out=acc[a, nb][:],
-                lhsT=x_codes[a // 2][:, c, rows].bitcast(E4M3X4 if c < PASSES - 1 else E5M2X4),
-                lhsT_scale=x_scales[a // 2][:, c, rows],
-                rhs=w_codes[:, c, cols].bitcast(E4M3X4),
-                rhs_scale=w_scales[:, c, cols],
-                start=(c == 0),
-                stop=(c == PASSES - 1),
-            )
+        def multiply(block, tiles, passes=range(PASSES)):
+            cols = slice(block * BLOCK, (block + 1) * BLOCK)
+            for c in passes:
+                for a in tiles:
+                    if c == 0:
+                        sums[a, block] = bank((a + 4) % TILES, [P, BLOCK])
+                    rows = slice((a % 2) * P, (a % 2 + 1) * P)
+                    nc.tensor.matmul_mx(
+                        out=sums[a, block][:],
+                        lhsT=x_codes[a // 2][:, c, rows].bitcast(E5M2X4 if c == Z_PASS else E4M3X4),
+                        lhsT_scale=x_scales[a // 2][:, c, rows],
+                        rhs=w_codes[:, c, cols].bitcast(E4M3X4),
+                        rhs_scale=w_scales[:, c, cols],
+                        start=(c == 0),
+                        stop=(c == PASSES - 1),
+                    )
 
-        y = {}
+        def empty(a, block, engine):
+            if block % 2 == 0:
+                y[a, block // 2] = y_pool.tile([P, HALF], F32, name="y")
+            first = (block % 2) * BLOCK
+            copy(engine, y[a, block // 2][:, first : first + BLOCK], sums[a, block][:])
 
-        def empty_acc(a, nb, eng):
-            if nb % 2 == 0:
-                y[a, nb // 2] = outs.tile([P, HALF], F32, name="y")
-            copy_cols(eng, y[a, nb // 2][:, (nb % 2) * NB:(nb % 2 + 1) * NB], acc[a, nb][:])
-
-        def copy_cols(eng, dst, src):
-            if eng == "V":
-                nc.vector.tensor_copy(out=dst, in_=src)
-            else:
-                nc.scalar.copy(out=dst, in_=src)
-
-        def store(a, h, lo, hi):
-            nc.sync.dma_start(out=out_rows[h][:, a, lo:hi], in_=y[a, h][:, lo:hi])
+        def store(a, half, first, end):
+            nc.sync.dma_start(out=out_rows[half][:, a, first:end], in_=y[a, half][:, first:end])
 
         def exp_row(a):
-            junk = stage.tile([P, HALF], BF16, name="junk_s")
-            nc.scalar.activation(out=junk[:], in_=y[a, 0][:], func=ACT.Exp, accum_out=exp_sums[:, a:a + 1])
+            junk = stage.tile([P, HALF], BF16, name="scalar_junk")
+            nc.scalar.activation(out=junk[:], in_=y[a, 0][:], func=ACT.Exp, accum_out=exp_sums[:, a : a + 1])
 
-        def square_row(a, i, eng):
-            square_cols(eng, y[a, 1][:, i * NB:(i + 1) * NB], sq_sums[:, i, a:a + 1])
-
-        def square_cols(eng, src, sums):
-            width = src.shape[1]
-            if eng == "V":
-                junk = stage.tile([P, NB], BF16, name="junk_v")
-                nc.vector.scalar_tensor_tensor(out=junk[:, 0:width], in0=src, scalar=1.0, in1=src, op0=ALU.mult, op1=ALU.mult, accum_out=sums)
+        def square(engine, values, row_sums):
+            if engine == VECTOR:
+                junk = stage.tile([P, BLOCK], BF16, name="vector_junk")
+                nc.vector.scalar_tensor_tensor(
+                    out=junk[:],
+                    in0=values,
+                    scalar=1.0,
+                    in1=values,
+                    op0=ALU.mult,
+                    op1=ALU.mult,
+                    accum_out=row_sums,
+                )
             else:
-                junk = stage.tile([P, HALF], BF16, name="junk_s")
-                nc.scalar.activation(out=junk[:, 0:width], in_=src, func=ACT.Square, accum_out=sums)
+                junk = stage.tile([P, HALF], BF16, name="scalar_junk")
+                nc.scalar.activation(out=junk[:, 0:BLOCK], in_=values, func=ACT.Square, accum_out=row_sums)
 
-        def mx(nb, tiles, cs=range(PASSES)):
-            for c in cs:
-                for a in tiles:
-                    product(a, nb, c)
+        def square_rows(a, i):
+            values = y[a, 1][:, i * BLOCK : (i + 1) * BLOCK]
+            square(VECTOR if a % 2 else SCALAR, values, square_sums[:, i, a : a + 1])
 
-        interleave_w(0, 0, 512)
-        quant_w(0, 0)
-        for pr in range(PAIRS):
-            transpose_pair(pr)
-            c0, c1, c2, c3 = T_ORDER[pr % 2]
-            if pr >= 2:
-                mx(0, (2 * pr - 4, 2 * pr - 3), (0,))
-            empty_t(pr, c0, "S")
-            empty_t(pr, c1, "V")
-            empty_t(pr, c2, "S")
-            empty_t(pr, c3, "S")
-            if pr == PAIRS - 1:
-                interleave_w(1, 0, 384)
-            quant_pair(pr)
-        quant_w(1, 0)
-        mx(0, (4, 5, 6, 7), (0,))
-        mx(0, range(TILES), (1,))
-        interleave_w(2, 0, 256)
-        interleave_w(3, 0, 256)
-        quant_w(2, 0)
-        mx(0, range(TILES), (2,))
-        interleave_w(0, 1, 256)
-        quant_w(3, 0)
-        mx(0, range(TILES), (3,))
-        interleave_w(1, 1, 256)
-        quant_w(0, 1)
-        interleave_w(2, 1, 256)
-        quant_w(1, 1)
-        interleave_w(3, 1, 256)
-        empty_acc(0, 0, "S")
-        empty_acc(1, 0, "V")
-        quant_w(2, 1)
-        empty_acc(2, 0, "S")
-        empty_acc(3, 0, "V")
-        quant_w(3, 1)
-        chain = [(0, 2), (0, 3), (1, 2), (2, 2), (3, 2), (1, 3), (2, 3), (3, 3)]
-        for a in range(4, TILES):
-            empty_acc(a, 0, "S")
-        interleave_w(*chain[0], 512)
-        mx(1, range(4))
-        for i in range(8):
-            if i + 1 < 8:
-                interleave_w(*chain[i + 1], 512)
-            quant_w(*chain[i])
+        group_w(0, 0, BLOCK)
+        quantise_w(0, 0)
+        for pair in range(PAIRS):
+            transpose_pair(pair)
+            if pair >= 2:
+                multiply(0, (2 * pair - 4, 2 * pair - 3), (0,))
+            engines = (VECTOR, SCALAR, SCALAR if pair % 2 else VECTOR, SCALAR)
+            for c, engine in zip(pass_order(pair), engines):
+                group_x(pair, c, engine)
+            if pair == PAIRS - 1:
+                group_w(1, 0, 384)
+            quantise_x(pair)
+        quantise_w(1, 0)
+        multiply(0, (4, 5, 6, 7), (0,))
+        multiply(0, range(TILES), (1,))
+
+        def empty_first(tiles):
+            for a in tiles:
+                empty(a, 0, VECTOR if a % 4 == 1 else SCALAR)
+
+        run = [(2, 0), (3, 0), (0, 1), (1, 1), (2, 1), (3, 1)]
+        group_w(*run[0], 256)
+        for i, (c, block) in enumerate(run):
+            if i + 1 < len(run):
+                group_w(*run[i + 1], 384 if i + 2 == len(run) else 256)
+            if i == 4:
+                empty_first(range(0, 4))
+            quantise_w(c, block)
+            if block == 0:
+                multiply(0, range(TILES), (c,))
+        empty_first(range(4, TILES))
+
+        multiply(1, range(2))
         for a in range(TILES):
-            if a >= 4:
-                mx(1, (a,))
-            empty_acc(a, 1, "S")
+            if a >= 2:
+                multiply(1, (a,))
+            empty(a, 1, SCALAR)
             store(a, 0, 0, HALF)
-            if a % 2 == 1:
+            if a >= 1:
                 exp_row(a - 1)
-                exp_row(a)
-        mx(2, range(4))
+
+        run = [(0, 2), (0, 3), (1, 2), (2, 2), (3, 2), (1, 3), (2, 3), (3, 3)]
+        group_w(*run[0], BLOCK)
+        for i, (c, block) in enumerate(run):
+            if i + 1 < len(run):
+                group_w(*run[i + 1], BLOCK)
+            quantise_w(c, block)
+
+        multiply(2, range(6))
         for a in range(TILES):
+            if a >= 6:
+                multiply(2, (a,))
+            empty(a, 2, VECTOR if a in (3, 5, 7) else SCALAR)
+            store(a, 1, 0, BLOCK)
+            if a == 0:
+                exp_row(TILES - 1)
             if a >= 4:
-                mx(2, (a,))
-            empty_acc(a, 2, "S" if a < 4 else "V")
-            store(a, 1, 0, NB)
+                square_rows(a - 4, 0)
 
         energy = keep.tile([P, TILES], F32, name="energy")
-        virtual = keep.tile([P, TILES], F32, name="virtual")
+        minus_energy = keep.tile([P, TILES], F32, name="minus_energy")
         total = keep.tile([P, TILES], F32, name="total")
+        virtual = keep.tile([P, TILES], F32, name="virtual")
         result = keep.tile([P, TILES], F32, name="result")
-        nc.scalar.activation(out=energy[:], in_=exp_sums[:], func=ACT.Ln)
-
-        def finish(lo, hi):
-            cols = slice(lo, hi)
-            if hi == TILES:
-                nc.vector.scalar_tensor_tensor(out=total[:, cols], in0=sq_sums[:, 0, cols], scalar=sq_sums[:, 2, cols], in1=sq_sums[:, 1, cols], op0=ALU.add, op1=ALU.add)
-            else:
-                nc.vector.tensor_add(out=total[:, cols], in0=sq_sums[:, 0, cols], in1=sq_sums[:, 1, cols])
-            nc.gpsimd.tensor_tensor(out=virtual[:, cols], in0=total[:, cols], in1=halves[:, cols], op=ALU.pow)
-            nc.gpsimd.tensor_tensor(out=result[:, cols], in0=virtual[:, cols], in1=energy[:, cols], op=ALU.subtract)
-
-        for a in range(TILES - 1):
-            mx(3, (a,))
-            mine, other = ("V", "S") if a % 2 == 0 else ("S", "V")
-            square_row(a, 0, other)
-            empty_acc(a, 3, mine)
-            store(a, 1, NB, HALF)
-            if a > 0:
-                square_row(a - 1, 1, mine)
-            if a >= 5:
-                finish(4 * (a - 5), 2 * a - 6)
         last = TILES - 1
-        mx(3, (last,))
-        square_row(last, 0, "V")
-        square_row(last - 1, 1, "S")
-        finish(last - 1, last)
-        src = acc[last, 3]
-        for eng, lo, hi in (("V", 0, NB // 2), ("S", NB // 2, NB)):
-            copy_cols(eng, y[last, 1][:, NB + lo:NB + hi], src[:, lo:hi])
-            store(last, 1, NB + lo, NB + hi)
-        square_cols("V", y[last, 1][:, NB:NB + NB // 2], sq_sums[:, 2, last:last + 1])
-        square_cols("S", y[last, 1][:, NB + NB // 2:HALF], sq_sums[:, 1, last:last + 1])
-        finish(last, TILES)
+        for a in range(last):
+            multiply(3, (a,))
+            if a == 1:
+                nc.scalar.activation(out=energy[:], in_=exp_sums[:], func=ACT.Ln)
+                nc.scalar.activation(out=unused[:], in_=one[:], func=ACT.Sqrt)
+                nc.gpsimd.tensor_scalar(
+                    out=minus_energy[:], in0=energy[:], scalar1=-1.0, scalar2=0.0, op0=ALU.mult, op1=ALU.add
+                )
+            empty(a, 3, SCALAR if a in (4, 6) else VECTOR)
+            store(a, 1, BLOCK, HALF)
+            if a + 4 < TILES:
+                square_rows(a + 4, 0)
+            if a >= 1:
+                square_rows(a - 1, 1)
+        multiply(3, (last,))
+        square_rows(last - 1, 1)
+        square(SCALAR, sums[last, 3][:], square_sums[:, 1, last:])
+        for first in (0, BLOCK // 2):
+            end = first + BLOCK // 2
+            copy(VECTOR, y[last, 1][:, BLOCK + first : BLOCK + end], sums[last, 3][:, first:end])
+            store(last, 1, BLOCK + first, BLOCK + end)
+        nc.scalar.activation(
+            out=virtual[:, last:],
+            in_=square_sums[:, 0, last:],
+            func=ACT.Sqrt,
+            bias=square_sums[:, 1, last:],
+        )
+        nc.scalar.activation(
+            out=result[:, last:], in_=virtual[:, last:], func=ACT.Identity, bias=minus_energy[:, last:]
+        )
+        nc.vector.tensor_add(out=total[:, 0:last], in0=square_sums[:, 0, 0:last], in1=square_sums[:, 1, 0:last])
+        nc.scalar.activation(out=virtual[:, 0:last], in_=total[:, 0:last], func=ACT.Sqrt)
+        nc.vector.tensor_add(out=result[:, 0:last], in0=virtual[:, 0:last], in1=minus_energy[:, 0:last])
         nc.sync.dma_start(out=score_rows, in_=result[:])

@@ -94,6 +94,7 @@ def tile_vim_ood_score_s2_kernel(tc, x, z, wx, wz, logits, resid, score):
         w_scales = keep.tile([P, PASSES, N], U8, name="w_scales", align_bytes=64)
         exp_sums = keep.tile([P, TILES], F32, name="exp_sums")
         square_sums = keep.tile([P, 2, TILES], F32, name="square_sums")
+        nc.vector.memset(square_sums[:], 0.0)
 
         def bank(i, shape):
             return psum.tile(shape, F32, name=f"bank{i}")
@@ -193,10 +194,11 @@ def tile_vim_ood_score_s2_kernel(tc, x, z, wx, wz, logits, resid, score):
             nc.scalar.activation(out=junk[:], in_=y[a, 0][:], func=ACT.Exp, accum_out=exp_sums[:, a : a + 1])
 
         def square(engine, values, row_sums):
+            width = values.shape[1]
             if engine == VECTOR:
-                junk = stage.tile([P, BLOCK], BF16, name="vector_junk")
+                junk = stage.tile([P, HALF], BF16, name="vector_junk")
                 nc.vector.scalar_tensor_tensor(
-                    out=junk[:],
+                    out=junk[:, 0:width],
                     in0=values,
                     scalar=1.0,
                     in1=values,
@@ -206,11 +208,7 @@ def tile_vim_ood_score_s2_kernel(tc, x, z, wx, wz, logits, resid, score):
                 )
             else:
                 junk = stage.tile([P, HALF], BF16, name="scalar_junk")
-                nc.scalar.activation(out=junk[:, 0:BLOCK], in_=values, func=ACT.Square, accum_out=row_sums)
-
-        def square_rows(a, i):
-            values = y[a, 1][:, i * BLOCK : (i + 1) * BLOCK]
-            square(VECTOR if a % 2 else SCALAR, values, square_sums[:, i, a : a + 1])
+                nc.scalar.activation(out=junk[:, 0:width], in_=values, func=ACT.Square, accum_out=row_sums)
 
         group_w(0, 0, BLOCK)
         quantise_w(0, 0)
@@ -218,7 +216,7 @@ def tile_vim_ood_score_s2_kernel(tc, x, z, wx, wz, logits, resid, score):
             transpose_pair(pair)
             if pair >= 2:
                 multiply(0, (2 * pair - 4, 2 * pair - 3), (0,))
-            engines = (VECTOR, SCALAR, SCALAR if pair % 2 else VECTOR, SCALAR)
+            engines = (VECTOR, SCALAR, SCALAR, SCALAR) if pair % 2 else (SCALAR, SCALAR, VECTOR, SCALAR)
             for c, engine in zip(pass_order(pair), engines):
                 group_x(pair, c, engine)
             if pair == PAIRS - 1:
@@ -228,21 +226,16 @@ def tile_vim_ood_score_s2_kernel(tc, x, z, wx, wz, logits, resid, score):
         multiply(0, (4, 5, 6, 7), (0,))
         multiply(0, range(TILES), (1,))
 
-        def empty_first(tiles):
-            for a in tiles:
-                empty(a, 0, VECTOR if a % 4 == 1 else SCALAR)
-
         run = [(2, 0), (3, 0), (0, 1), (1, 1), (2, 1), (3, 1)]
-        group_w(*run[0], 256)
+        group_w(*run[0], BLOCK // 2)
         for i, (c, block) in enumerate(run):
             if i + 1 < len(run):
-                group_w(*run[i + 1], 384 if i + 2 == len(run) else 256)
-            if i == 4:
-                empty_first(range(0, 4))
+                group_w(*run[i + 1], BLOCK if i + 2 == len(run) else BLOCK // 2)
             quantise_w(c, block)
             if block == 0:
                 multiply(0, range(TILES), (c,))
-        empty_first(range(4, TILES))
+        for a in range(TILES):
+            empty(a, 0, SCALAR)
 
         multiply(1, range(2))
         for a in range(TILES):
@@ -250,8 +243,8 @@ def tile_vim_ood_score_s2_kernel(tc, x, z, wx, wz, logits, resid, score):
                 multiply(1, (a,))
             empty(a, 1, SCALAR)
             store(a, 0, 0, HALF)
-            if a >= 1:
-                exp_row(a - 1)
+            if a >= 2:
+                exp_row(a - 2)
 
         run = [(0, 2), (0, 3), (1, 2), (2, 2), (3, 2), (1, 3), (2, 3), (3, 3)]
         group_w(*run[0], BLOCK)
@@ -264,12 +257,10 @@ def tile_vim_ood_score_s2_kernel(tc, x, z, wx, wz, logits, resid, score):
         for a in range(TILES):
             if a >= 6:
                 multiply(2, (a,))
-            empty(a, 2, VECTOR if a in (3, 5, 7) else SCALAR)
+            empty(a, 2, SCALAR if a < 4 else VECTOR)
             store(a, 1, 0, BLOCK)
-            if a == 0:
-                exp_row(TILES - 1)
-            if a >= 4:
-                square_rows(a - 4, 0)
+            if a < 2:
+                exp_row(TILES - 2 + a)
 
         energy = keep.tile([P, TILES], F32, name="energy")
         minus_energy = keep.tile([P, TILES], F32, name="minus_energy")
@@ -279,7 +270,7 @@ def tile_vim_ood_score_s2_kernel(tc, x, z, wx, wz, logits, resid, score):
         last = TILES - 1
         for a in range(last):
             multiply(3, (a,))
-            if a == 1:
+            if a == 0:
                 nc.scalar.activation(out=energy[:], in_=exp_sums[:], func=ACT.Ln)
                 nc.scalar.activation(out=unused[:], in_=one[:], func=ACT.Sqrt)
                 nc.gpsimd.tensor_scalar(
@@ -287,12 +278,13 @@ def tile_vim_ood_score_s2_kernel(tc, x, z, wx, wz, logits, resid, score):
                 )
             empty(a, 3, SCALAR if a in (4, 6) else VECTOR)
             store(a, 1, BLOCK, HALF)
-            if a + 4 < TILES:
-                square_rows(a + 4, 0)
+            if a == 4:
+                square(SCALAR, y[last - 1, 1][:, 0:BLOCK], square_sums[:, 0, last - 1 : last])
+                square(VECTOR, y[last, 1][:, 0:BLOCK], square_sums[:, 0, last:])
             if a >= 1:
-                square_rows(a - 1, 1)
+                square(SCALAR if a % 2 == 0 else VECTOR, y[a - 1, 1][:], square_sums[:, 0, a - 1 : a])
         multiply(3, (last,))
-        square_rows(last - 1, 1)
+        square(VECTOR, y[last - 1, 1][:, BLOCK:], square_sums[:, 1, last - 1 : last])
         square(SCALAR, sums[last, 3][:], square_sums[:, 1, last:])
         for first in (0, BLOCK // 2):
             end = first + BLOCK // 2

from contextlib import ExitStack

import concourse.mybir as mybir
from concourse.masks import make_identity

M = 1024
K1, K2 = 1536, 512
HALF = 1024
N = 2 * HALF
FLOPS = 2 * M * (K1 + K2) * N

F32 = mybir.dt.float32
BF16 = mybir.dt.bfloat16
U32 = mybir.dt.uint32
U8 = mybir.dt.uint8
E4M3X4 = mybir.dt.float8_e4m3fn_x4
E5M2X4 = mybir.dt.float8_e5m2_x4
ACT = mybir.ActivationFunctionType
ALU = mybir.AluOpType

P = 128
PACK = 4
K_PASS = P * PACK
PASSES = (K1 + K2) // K_PASS
Z_PASS = PASSES - 1
TILES = M // P
PAIRS = TILES // 2
BLOCK = 512
VECTOR, SCALAR = "vector", "scalar"


def tile_vim_ood_score_s2_kernel(tc, x, z, wx, wz, logits, resid, score):
    nc = tc.nc

    x_rows = x.rearrange("(p a) k -> p a k", a=TILES)
    z_rows = z.rearrange("(p a) k -> p a k", a=TILES)
    out_rows = [y.rearrange("(p a) n -> p a n", a=TILES) for y in (logits, resid)]
    score_rows = score.rearrange("(p a) o -> p (a o)", a=TILES)

    with ExitStack() as ctx:
        keep = ctx.enter_context(tc.tile_pool(name="keep", bufs=1))
        w_pool = ctx.enter_context(tc.tile_pool(name="w_pool", bufs=1))
        stage = ctx.enter_context(tc.tile_pool(name="stage", bufs=2))
        y_pool = ctx.enter_context(tc.tile_pool(name="y_pool", bufs=10))
        psum = ctx.enter_context(tc.psum_pool(name="psum", bufs=1))
        ctx.enter_context(tc.manual_schedule())

        x_raw, z_raw, w_raw = {}, {}, {}

        def load_x(pair):
            raw = keep.tile([P, 2, K1], BF16, name=f"x_raw{pair}", align_bytes=64)
            nc.sync.dma_start(out=raw[:], in_=x_rows[:, 2 * pair : 2 * pair + 2, :])
            x_raw[pair] = raw

        def load_z(pair):
            raw = keep.tile([P, 4, K2], BF16, name=f"z_raw{pair}", align_bytes=64)
            nc.sync.dma_start(out=raw[:], in_=z_rows[:, 2 * pair : 2 * pair + 4, :])
            z_raw[pair], z_raw[pair + 1] = raw[:, 0:2, :], raw[:, 2:4, :]

        def load_w(c, block, blocks):
            rows = wz if c == Z_PASS else wx[c * K_PASS : (c + 1) * K_PASS, :]
            cols = slice(block * BLOCK, (block + blocks) * BLOCK)
            raw = w_pool.tile(
                [P, PACK, blocks * BLOCK], BF16, name=f"w_raw{blocks}", bufs=8 // blocks, align_bytes=64
            )
            nc.sync.dma_start(out=raw[:], in_=rows.rearrange("(p j) n -> p j n", j=PACK)[:, :, cols])
            for i in range(blocks):
                w_raw[c, block + i] = raw[:, :, i * BLOCK : (i + 1) * BLOCK]

        load_w(0, 0, 1)
        load_x(0)
        load_z(0)
        load_x(1)
        load_x(2)
        load_z(2)
        load_x(3)
        for c in range(1, PASSES):
            load_w(c, 0, 1)
        for c in range(PASSES):
            load_w(c, 1, 1)
        for c in range(PASSES):
            load_w(c, 2, 2)

        identity = keep.tile([P, P], F32, name="identity")
        make_identity(nc, identity[:])
        one = keep.tile([P, 1], F32, name="one")
        nc.vector.memset(one[:], 1.0)
        unused = keep.tile([P, 1], F32, name="unused")
        nc.scalar.activation(out=unused[:], in_=one[:], func=ACT.Exp)

        x_codes = [keep.tile([P, PASSES, 2 * P], U32, name=f"x_codes{i}", align_bytes=64) for i in range(PAIRS)]
        x_scales = [keep.tile([P, PASSES, 2 * P], U8, name=f"x_scales{i}", align_bytes=64) for i in range(PAIRS)]
        w_codes = keep.tile([P, PASSES, N], U32, name="w_codes", align_bytes=64)
        w_scales = keep.tile([P, PASSES, N], U8, name="w_scales", align_bytes=64)
        exp_sums = keep.tile([P, TILES], F32, name="exp_sums")
        square_sums = keep.tile([P, 2, TILES], F32, name="square_sums")
        nc.vector.memset(square_sums[:], 0.0)

        def bank(i, shape):
            return psum.tile(shape, F32, name=f"bank{i}")

        def copy(engine, out, in_):
            if engine == VECTOR:
                nc.vector.tensor_copy(out=out, in_=in_)
            else:
                nc.scalar.copy(out=out, in_=in_)

        transposed, x_grouped = {}, {}

        def pass_order(pair):
            return (0, 1, 2, Z_PASS) if pair % 2 == 0 else (Z_PASS, 0, 1, 2)

        def transpose_pair(pair):
            for i, c in enumerate(pass_order(pair)):
                out = bank(i, [P, 2, 2, P])
                raw, first_k = (z_raw[pair], 0) if c == Z_PASS else (x_raw[pair], c * K_PASS)
                for a in range(2):
                    words = raw[:, a, first_k : first_k + K_PASS].bitcast(F32)
                    for u in range(2):
                        nc.tensor.transpose(out[:, a, u, :], words[:, u::2], identity[:])
                transposed[pair, c] = out

        def group_x(pair, c, engine):
            half = c // 2
            if (pair, half) not in x_grouped:
                grouped = stage.tile([P, 2, 2 * P * PACK], BF16, name=f"x_grouped{half}", align_bytes=64)
                x_grouped[pair, half] = grouped
            words = x_grouped[pair, half][:, c % 2, :].bitcast(F32)
            copy(
                engine,
                out=words.rearrange("p (a m u) -> p a m u", a=2, u=2),
                in_=transposed[pair, c][:].rearrange("p a u m -> p a m u"),
            )

        def quantise_x(pair):
            for first, end, fmt in ((0, 2, E4M3X4), (2, Z_PASS, E4M3X4), (Z_PASS, PASSES, E5M2X4)):
                grouped = x_grouped[pair, first // 2][:, first % 2 : first % 2 + end - first, :]
                nc.vector.quantize_mx(
                    out=x_codes[pair][:, first:end, :].rearrange("p c m -> p (c m)").bitcast(fmt),
                    scales=x_scales[pair][:, first:end, :].rearrange("p c m -> p (c m)"),
                    in_=grouped.rearrange("p c q -> p (c q)"),
                )

        w_grouped = {}

        def group_w(c, block, vector_cols):
            grouped = stage.tile([P, BLOCK, PACK], BF16, name="w_grouped", bufs=4, align_bytes=64)
            w_grouped[c, block] = grouped
            src = w_raw[c, block].rearrange("p j (n i) -> p n j i", i=4)
            dst = grouped[:].rearrange("p (n i) j -> p n j i", i=4)
            cut = vector_cols // 4
            copy(VECTOR, dst[:, 0:cut], src[:, 0:cut])
            if vector_cols < BLOCK:
                copy(SCALAR, dst[:, cut:], src[:, cut:])

        def quantise_w(c, block):
            cols = slice(block * BLOCK, (block + 1) * BLOCK)
            nc.vector.quantize_mx(
                out=w_codes[:, c, cols].bitcast(E4M3X4),
                scales=w_scales[:, c, cols],
                in_=w_grouped[c, block][:].rearrange("p n j -> p (n j)"),
            )

        sums, y = {}, {}

        def multiply(block, tiles, passes=range(PASSES)):
            cols = slice(block * BLOCK, (block + 1) * BLOCK)
            for c in passes:
                for a in tiles:
                    if c == 0:
                        sums[a, block] = bank((a + 4) % TILES, [P, BLOCK])
                    rows = slice((a % 2) * P, (a % 2 + 1) * P)
                    nc.tensor.matmul_mx(
                        out=sums[a, block][:],
                        lhsT=x_codes[a // 2][:, c, rows].bitcast(E5M2X4 if c == Z_PASS else E4M3X4),
                        lhsT_scale=x_scales[a // 2][:, c, rows],
                        rhs=w_codes[:, c, cols].bitcast(E4M3X4),
                        rhs_scale=w_scales[:, c, cols],
                        start=(c == 0),
                        stop=(c == PASSES - 1),
                    )

        def empty(a, block, engine):
            if block % 2 == 0:
                y[a, block // 2] = y_pool.tile([P, HALF], F32, name="y")
            first = (block % 2) * BLOCK
            copy(engine, y[a, block // 2][:, first : first + BLOCK], sums[a, block][:])

        def store(a, half, first, end):
            nc.sync.dma_start(out=out_rows[half][:, a, first:end], in_=y[a, half][:, first:end])

        def exp_row(a):
            junk = stage.tile([P, HALF], BF16, name="scalar_junk")
            nc.scalar.activation(out=junk[:], in_=y[a, 0][:], func=ACT.Exp, accum_out=exp_sums[:, a : a + 1])

        def square(engine, values, row_sums):
            width = values.shape[1]
            if engine == VECTOR:
                junk = stage.tile([P, HALF], BF16, name="vector_junk")
                nc.vector.scalar_tensor_tensor(
                    out=junk[:, 0:width],
                    in0=values,
                    scalar=1.0,
                    in1=values,
                    op0=ALU.mult,
                    op1=ALU.mult,
                    accum_out=row_sums,
                )
            else:
                junk = stage.tile([P, HALF], BF16, name="scalar_junk")
                nc.scalar.activation(out=junk[:, 0:width], in_=values, func=ACT.Square, accum_out=row_sums)

        group_w(0, 0, BLOCK)
        quantise_w(0, 0)
        for pair in range(PAIRS):
            transpose_pair(pair)
            if pair >= 2:
                multiply(0, (2 * pair - 4, 2 * pair - 3), (0,))
            engines = (VECTOR, SCALAR, SCALAR, SCALAR) if pair % 2 else (SCALAR, SCALAR, VECTOR, SCALAR)
            for c, engine in zip(pass_order(pair), engines):
                group_x(pair, c, engine)
            if pair == PAIRS - 1:
                group_w(1, 0, 384)
            quantise_x(pair)
        quantise_w(1, 0)
        multiply(0, (4, 5, 6, 7), (0,))
        multiply(0, range(TILES), (1,))

        run = [(2, 0), (3, 0), (0, 1), (1, 1), (2, 1), (3, 1)]
        group_w(*run[0], BLOCK // 2)
        for i, (c, block) in enumerate(run):
            if i + 1 < len(run):
                group_w(*run[i + 1], BLOCK if i + 2 == len(run) else BLOCK // 2)
            quantise_w(c, block)
            if block == 0:
                multiply(0, range(TILES), (c,))
        for a in range(TILES):
            empty(a, 0, SCALAR)

        multiply(1, range(2))
        for a in range(TILES):
            if a >= 2:
                multiply(1, (a,))
            empty(a, 1, SCALAR)
            store(a, 0, 0, HALF)
            if a >= 2:
                exp_row(a - 2)

        run = [(0, 2), (0, 3), (1, 2), (2, 2), (3, 2), (1, 3), (2, 3), (3, 3)]
        group_w(*run[0], BLOCK)
        for i, (c, block) in enumerate(run):
            if i + 1 < len(run):
                group_w(*run[i + 1], BLOCK)
            quantise_w(c, block)

        multiply(2, range(6))
        for a in range(TILES):
            if a >= 6:
                multiply(2, (a,))
            empty(a, 2, SCALAR if a < 4 else VECTOR)
            store(a, 1, 0, BLOCK)
            if a < 2:
                exp_row(TILES - 2 + a)

        energy = keep.tile([P, TILES], F32, name="energy")
        minus_energy = keep.tile([P, TILES], F32, name="minus_energy")
        total = keep.tile([P, TILES], F32, name="total")
        virtual = keep.tile([P, TILES], F32, name="virtual")
        result = keep.tile([P, TILES], F32, name="result")
        last = TILES - 1
        for a in range(last):
            multiply(3, (a,))
            if a == 0:
                nc.scalar.activation(out=energy[:], in_=exp_sums[:], func=ACT.Ln)
                nc.scalar.activation(out=unused[:], in_=one[:], func=ACT.Sqrt)
                nc.gpsimd.tensor_scalar(
                    out=minus_energy[:], in0=energy[:], scalar1=-1.0, scalar2=0.0, op0=ALU.mult, op1=ALU.add
                )
            empty(a, 3, SCALAR if a in (4, 6) else VECTOR)
            store(a, 1, BLOCK, HALF)
            if a == 4:
                square(SCALAR, y[last - 1, 1][:, 0:BLOCK], square_sums[:, 0, last - 1 : last])
                square(VECTOR, y[last, 1][:, 0:BLOCK], square_sums[:, 0, last:])
            if a >= 1:
                square(SCALAR if a % 2 == 0 else VECTOR, y[a - 1, 1][:], square_sums[:, 0, a - 1 : a])
        multiply(3, (last,))
        square(VECTOR, y[last - 1, 1][:, BLOCK:], square_sums[:, 1, last - 1 : last])
        square(SCALAR, sums[last, 3][:], square_sums[:, 1, last:])
        for first in (0, BLOCK // 2):
            end = first + BLOCK // 2
            copy(VECTOR, y[last, 1][:, BLOCK + first : BLOCK + end], sums[last, 3][:, first:end])
            store(last, 1, BLOCK + first, BLOCK + end)
        nc.scalar.activation(
            out=virtual[:, last:],
            in_=square_sums[:, 0, last:],
            func=ACT.Sqrt,
            bias=square_sums[:, 1, last:],
        )
        nc.scalar.activation(
            out=result[:, last:], in_=virtual[:, last:], func=ACT.Identity, bias=minus_energy[:, last:]
        )
        nc.vector.tensor_add(out=total[:, 0:last], in0=square_sums[:, 0, 0:last], in1=square_sums[:, 1, 0:last])
        nc.scalar.activation(out=virtual[:, 0:last], in_=total[:, 0:last], func=ACT.Sqrt)
        nc.vector.tensor_add(out=result[:, 0:last], in0=virtual[:, 0:last], in1=minus_energy[:, 0:last])
        nc.sync.dma_start(out=score_rows, in_=result[:])
